import numpy as np
import ml_dtypes


def mxq(x, axis, fmt="e4m3"):
    dtype, down = {"e4m3": (ml_dtypes.float8_e4m3fn, 7), "e5m2": (ml_dtypes.float8_e5m2, 14)}[fmt]
    v = np.moveaxis(np.asarray(x, np.float32).astype(ml_dtypes.bfloat16).astype(np.float64), axis, -1)
    blocks = v.reshape(v.shape[:-1] + (-1, 32))
    amax = np.abs(blocks).max(-1, keepdims=True)
    byte = np.maximum(np.where(amax > 0, np.frexp(amax)[1] - 1 + 127, 0) - down, 1)
    scale = np.exp2(byte - 127.0)
    codes = (blocks / scale).astype(np.float32).astype(dtype).astype(np.float64)
    return np.moveaxis((codes * scale).reshape(v.shape), -1, axis)


WIDE = False


def mx_kscale(k):
    if not WIDE:
        return np.ones(k)
    levels = np.array([10, -10, 5, -5, 0])
    if k % 512:
        return np.exp2(np.random.permutation(np.resize(levels, k // 32))).repeat(32)
    a = np.empty((k // 512, 16))
    for p in range(k // 512):
        a[p, :8] = np.random.permutation(np.resize(levels, 8))
        for g in range(8):
            far = levels[np.abs(levels - a[p, g]) >= 10]
            a[p, g + 8] = far[np.random.randint(len(far))]
    return np.exp2(a.ravel()).repeat(32)


def f64(x):
    return np.asarray(x).astype(np.float64)


def striped(idx):
    return np.tile(idx.reshape(-1, 16).T, (8, 1)).astype(np.uint16)


def unstriped(offs):
    return offs[:16].T.reshape(-1).astype(np.int64)


E2M1 = np.array([0.0, 0.5, 1.0, 1.5, 2.0, 3.0, 4.0, 6.0, -0.0, -0.5, -1.0, -1.5, -2.0, -3.0, -4.0, -6.0])


def pack_weight(w, fmt):
    k, n = w.shape
    w = f64(np.asarray(w, np.float32).astype(ml_dtypes.bfloat16)).reshape(k // 32, 32, n)
    amax = np.abs(w).max(1)
    if fmt == "e4m3":
        byte = np.frexp(amax)[1] - 1 + 127 - 7
    else:
        mant, ex = np.frexp(amax / 6.0)
        byte = np.where(mant > 0.5, ex, ex - 1) + 127
    byte = np.clip(np.where(amax > 0, byte, 1), 1, 254)
    scaled = (w * np.exp2(127.0 - byte)[:, None, :]).reshape(k, n).astype(np.float32)
    by_word = np.ascontiguousarray(scaled.reshape(k // 512, 128, 4, n).transpose(0, 1, 3, 2))
    if fmt == "e4m3":
        words = by_word.astype(ml_dtypes.float8_e4m3fn).view(np.uint8)
    else:
        c = by_word.astype(ml_dtypes.float4_e2m1fn).view(np.uint8) & 0xF
        words = (c[..., 0::2] | (c[..., 1::2] << 4)).reshape(k // 512, 128, 2 * n)
    return np.ascontiguousarray(words), np.ascontiguousarray(byte.astype(np.uint8).reshape(k // 512, 16, n))


def unpack_weight(words, scales, fmt):
    g, _, n = scales.shape
    words = np.ascontiguousarray(words).reshape(g, 128, n, -1)
    if fmt == "e4m3":
        vals = words.view(ml_dtypes.float8_e4m3fn).astype(np.float64)
    else:
        nib = np.empty((g, 128, n, 4), np.uint8)
        nib[..., 0::2] = words & 0xF
        nib[..., 1::2] = words >> 4
        vals = E2M1[nib]
    vals = vals * np.repeat(np.exp2(scales.astype(np.float64) - 127.0), 8, axis=1)[..., None]
    return vals.transpose(0, 1, 3, 2).reshape(g * 512, n)


def gelu(v):
    return 0.5 * v * (1.0 + np.tanh(np.sqrt(2.0 / np.pi) * (v + 0.044715 * v**3)))


def bf(x):
    return np.asarray(x, np.float32).astype(ml_dtypes.bfloat16)


def planes(Y):
    n, m = Y.shape
    b = f64(bf(Y)).reshape(n // 32, 32, m)
    amax = np.abs(b).max(1)
    byte = np.clip(np.where(amax > 0, np.frexp(amax)[1] - 1 + 127 - 7, 1), 1, 254)
    codes = (b * np.exp2(127.0 - byte)[:, None, :]).reshape(n, m).astype(np.float32).astype(ml_dtypes.float8_e4m3fn).view(np.uint8)
    words = codes.reshape(n // 512, 128, 4, m).transpose(0, 1, 3, 2)
    return np.ascontiguousarray(words), np.ascontiguousarray(byte.astype(np.uint8).reshape(n // 512, 16, m))


K, T, S, H, P, N = 512, 4096, 1024, 1024, 512, 1024

def setup_inputs():
    n = np.random.standard_normal
    s = mx_kscale(K)[:, None]
    u = mx_kscale(H)[:, None]
    rs = np.exp(0.8 * n(N))
    d = {}
    d["tab_words"], d["tab_scales"] = pack_weight(n((K, T)) * s, "e4m3")
    d["offs"] = striped(np.random.permutation(T)[:S])
    d["pos1"] = striped(np.random.permutation(S)[:P])
    d["pos2"] = striped(np.random.permutation(S)[:P])
    d["w1"] = (0.5 * n((K, H)) / K ** 0.5 / s).astype(np.float32)
    d["w2_words"], d["w2_scales"] = pack_weight(1.6 * n((K, H)) / K ** 0.5 / s, "e2m1")
    d["gain"] = (np.exp(0.3 * n(H)) * u[:, 0]).astype(np.float32)
    d["w3"] = (1.2 * n((H, N)) / H ** 0.5 / u * rs[None, :]).astype(np.float32)
    d["base"] = (0.7 * n((N, S)) * rs[:, None]).astype(np.float32)
    return d

def reference(tab_words, tab_scales, offs, pos1, pos2, w1, w2_words, w2_scales, gain, w3, base):
    v = unpack_weight(tab_words, tab_scales, "e4m3")[:, unstriped(offs)]
    w2 = unpack_weight(w2_words, w2_scales, "e2m1")
    reach = mxq(f64(w1), 0, "e4m3").T @ v
    bulge = w2.T @ v
    near = 1.0 / (1.0 + np.abs(bulge))
    h = (reach - near) * f64(gain)[:, None]
    g2 = (mxq(f64(w3), 0, "e4m3").T @ mxq(h, 0, "e4m3")) + f64(base)
    y = np.maximum(g2[:, unstriped(pos1)], g2[:, unstriped(pos2)])
    words, scales = planes(y)
    return y, words, scales

@@ -1,0 +1,281 @@
+from contextlib import ExitStack
+
+import concourse.mybir as mybir
+
+K, T, S, H, M, N = 512, 4096, 1024, 1024, 512, 1024
+FLOPS = 2 * (2 * K * H * S + H * N * S)
+
+F32 = mybir.dt.float32
+BF16 = mybir.dt.bfloat16
+I32 = mybir.dt.int32
+U32 = mybir.dt.uint32
+U16 = mybir.dt.uint16
+U8 = mybir.dt.uint8
+FP8X4 = mybir.dt.float8_e4m3fn_x4
+FP4X4 = mybir.dt.float4_e2m1fn_x4
+ALU = mybir.AluOpType
+ACT = mybir.ActivationFunctionType
+
+P = 128
+PASS = 512
+BANK = 512
+UNIT = 256
+
+
+def tile_list_flank_brush_features_kernel(
+    tc, tab_words, tab_scales, offs, pos1, pos2, w1, w2_words, w2_scales, gain, w3, base, out_0, out_1, out_2
+):
+    nc = tc.nc
+    with ExitStack() as ctx:
+        keep = ctx.enter_context(tc.tile_pool(name="keep", bufs=1))
+        big = ctx.enter_context(tc.tile_pool(name="big", bufs=1))
+        ring = ctx.enter_context(tc.tile_pool(name="ring", bufs=2))
+        psum = ctx.enter_context(tc.psum_pool(name="psum", bufs=1))
+
+        def load_scale_rows(tile, rows, queues):
+            for q in range(4):
+                queues[q].dma_start(out=tile[32 * q : 32 * q + 4, :].bitcast(I32), in_=rows[4 * q : 4 * q + 4, :].bitcast(I32))
+
+        offs_t = keep.tile([P, S // 16], U16, name="offs_t")
+        pos1_t = keep.tile([P, M // 16], U16, name="pos1_t")
+        pos2_t = keep.tile([P, M // 16], U16, name="pos2_t")
+        w2s_raw = big.tile([P, H], U8, name="w2s_raw", tag="d", align_bytes=64)
+        tabs = big.tile([P, T], U8, name="tabs", tag="b", align_bytes=64)
+        nc.gpsimd.memset(w2s_raw[:].bitcast(I32), 0)
+        nc.gpsimd.memset(tabs[:, : T // 2].bitcast(I32), 0)
+        nc.vector.memset(tabs[:, T // 2 :].bitcast(I32), 0)
+        w2w_raw = big.tile([P, 2 * H], U8, name="w2w_raw", tag="c", align_bytes=64)
+        gain_t = keep.tile([P, 2, 4], F32, name="gain_t")
+        tabw = big.tile([P, T], I32, name="tabw", tag="a", align_bytes=64)
+        load_scale_rows(w2s_raw, w2_scales[0], [nc.scalar, nc.scalar, nc.scalar, nc.sync])
+        nc.sync.dma_start(offs_t[:], offs)
+        nc.sync.dma_start(out=w2w_raw[:].bitcast(I32), in_=w2_words[0].bitcast(I32))
+        nc.sync.dma_start(out=tabw[:], in_=tab_words[0].rearrange("p n t -> p (n t)").bitcast(I32))
+        load_scale_rows(tabs, tab_scales[0], [nc.sync] * 4)
+        nc.sync.dma_start(pos1_t[:], pos1)
+        nc.sync.dma_start(pos2_t[:], pos2)
+        nc.gpsimd.dma_start(out=gain_t[:], in_=gain.rearrange("(b p t) -> p b t", b=2, t=4))
+
+        def load_weight(tile, rows):
+            nc.sync.dma_start(out=tile, in_=rows.rearrange("(p j) c -> p j c", j=4))
+
+        def load_w3(g, tag):
+            raw = big.tile([P, 2, 4, PASS], F32, name="w3_raw%d" % g, tag=tag, align_bytes=64)
+            for b in range(2):
+                load_weight(raw[:, b], w3[b * PASS : (b + 1) * PASS, g * PASS : (g + 1) * PASS])
+            return raw
+
+        def load_base(g, tag):
+            tile = big.tile([P, 4 * S], F32, name="page%d" % g, tag=tag, align_bytes=64)
+            nc.sync.dma_start(out=tile[:], in_=base[g * PASS : (g + 1) * PASS, :].rearrange("(p t) j -> p (t j)", t=4))
+            return tile
+
+        w2w = keep.tile([P, 2 * H], U8, name="w2w", align_bytes=64)
+        w2s = keep.tile([P, H], U8, name="w2s", align_bytes=64)
+        for b in range(2):
+            nc.vector.tensor_copy(
+                out=w2w[:, 2 * b * PASS : 2 * (b + 1) * PASS].rearrange("p (t m e) -> p m t e", t=4, e=2),
+                in_=w2w_raw[:, 2 * b * PASS : 2 * (b + 1) * PASS].rearrange("p (m t e) -> p m t e", t=4, e=2),
+            )
+        nc.vector.tensor_copy(
+            out=w2s[:].rearrange("p (b t m) -> p b m t", b=2, t=4),
+            in_=w2s_raw[:].rearrange("p (b m t) -> p b m t", b=2, t=4),
+        )
+
+        w1_raw = []
+        for b in range(2):
+            raw = big.tile([P, 4, PASS], F32, name="w1_raw%d" % b, tag="cd"[b], align_bytes=64)
+            load_weight(raw[:], w1[:, b * PASS : (b + 1) * PASS])
+            w1_raw.append(raw)
+
+        vw, vs = {}, {}
+
+        def gather_table(jh):
+            words = big.tile([P, BANK], U32, name="vw%d" % jh, tag="ef"[jh], align_bytes=64)
+            scales = keep.tile([P, BANK], U8, name="vs%d" % jh, align_bytes=64)
+            lst = offs_t[:, jh * 32 : (jh + 1) * 32]
+            nc.vector.tensor_copy(out=words[:], in_=tabw[:].bitcast(U32).indirect(lst))
+            nc.vector.tensor_copy(out=scales[:], in_=tabs[:].indirect(lst))
+            vw[jh] = words
+            vs[jh] = scales
+
+        def staging(pool, tag):
+            tile = pool.tile([P, 4 * PASS], BF16, name="grouped", tag=tag, align_bytes=64)
+            return tile[:]
+
+        def quantize_weight(raw, name, copy, grouped):
+            copy(
+                out=grouped.rearrange("p (t m j) -> p m j t", t=4, j=4),
+                in_=raw.rearrange("p j (m t) -> p m j t", t=4),
+            )
+            codes = keep.tile([P, PASS], U32, name=name + "_codes", align_bytes=64)
+            scales = keep.tile([P, PASS], U8, name=name + "_scales", align_bytes=64)
+            nc.vector.quantize_mx(out=codes[:].bitcast(FP8X4), scales=scales[:], in_=grouped)
+            return codes, scales
+
+        gather_table(0)
+        w1q = [quantize_weight(w1_raw[0][:], "w1q0", nc.vector.tensor_copy, staging(big, "f"))]
+        gather_table(1)
+        w1q.append(quantize_weight(w1_raw[1][:], "w1q1", nc.vector.tensor_copy, staging(ring, "grouped")))
+        w3_raw = [load_w3(0, "a")]
+        pages = [load_base(0, "b"), load_base(1, "c")]
+        w3_raw.append(load_w3(1, "d"))
+        page = {(g, t): pages[g][:, t * S : (t + 1) * S] for g in range(2) for t in range(4)}
+
+        hw = {}
+        hs = {}
+        for jh in range(2):
+            for b in range(2):
+                hw[jh, b] = keep.tile([P, BANK], U32, name="hw%d%d" % (jh, b), align_bytes=64)
+                hs[jh, b] = keep.tile([P, BANK], U8, name="hs%d%d" % (jh, b), align_bytes=64)
+
+        sqs = [keep.tile([P, 4 * UNIT], F32, name="sq%d" % b, align_bytes=64) for b in range(2)]
+        nears = [keep.tile([P, 4 * UNIT], F32, name="near%d" % b, align_bytes=64) for b in range(2)]
+
+        units = [(jh, u, b) for jh in range(2) for u in range(BANK // UNIT) for b in range(2)]
+        mags, diffs, hbf = {}, {}, {}
+
+        def blocks(u):
+            return [slice(u * UNIT + i * P, u * UNIT + (i + 1) * P) for i in range(UNIT // P)]
+
+        def four_products(bank, words, dtype, width, scales, jh, cols):
+            for t in range(4):
+                nc.tensor.matmul_mx(
+                    out=bank[:, t * P : (t + 1) * P],
+                    lhsT=words[:, width * t * P : width * (t + 1) * P].bitcast(dtype),
+                    lhsT_scale=scales[:, t * P : (t + 1) * P],
+                    rhs=vw[jh][:, cols].bitcast(FP8X4),
+                    rhs_scale=vs[jh][:, cols],
+                    start=True,
+                    stop=True,
+                )
+
+        def magnitude(n):
+            jh, u, b = units[n]
+            mag = ring.tile([P, 4 * UNIT], F32, name="mag")
+            for i, cols in enumerate(blocks(u)):
+                bulge = psum.tile([P, BANK], F32, name="bulge", bufs=3)
+                four_products(bulge, w2w[:, 2 * b * PASS : 2 * (b + 1) * PASS], FP4X4, 2, w2s[:, b * PASS : (b + 1) * PASS], jh, cols)
+                nc.scalar.activation(
+                    out=mag[:, i * BANK : (i + 1) * BANK].rearrange("p (j t) -> p j t", t=4),
+                    in_=bulge[:].rearrange("p (t j) -> p j t", t=4),
+                    func=ACT.Abs,
+                )
+            mags[n] = mag
+
+        def square(n):
+            nc.scalar.activation(out=sqs[n % 2][:], in_=mags[n][:], func=ACT.Square, bias=1.0)
+
+        def nearness(n):
+            nc.scalar.activation(out=nears[n % 2][:], in_=sqs[n % 2][:], func=ACT.Abs_reciprocal_sqrt)
+
+        def difference(n):
+            jh, u, b = units[n]
+            diff = ring.tile([P, 4 * UNIT], F32, name="diff")
+            codes, scales = w1q[b]
+            for i, cols in enumerate(blocks(u)):
+                reach = psum.tile([P, BANK], F32, name="reach", bufs=3)
+                four_products(reach, codes, FP8X4, 1, scales, jh, cols)
+                nc.vector.tensor_tensor(
+                    out=diff[:, i * BANK : (i + 1) * BANK].rearrange("p (j t) -> p j t", t=4),
+                    in0=reach[:].rearrange("p (t j) -> p j t", t=4),
+                    in1=nears[n % 2][:, i * BANK : (i + 1) * BANK].rearrange("p (j t) -> p j t", t=4),
+                    op=ALU.subtract,
+                )
+            diffs[n] = diff
+
+        def apply_gain(n):
+            b = units[n][2]
+            h = ring.tile([P, 4 * UNIT], BF16, name="h", align_bytes=64)
+            nc.vector.tensor_tensor(
+                out=h[:].rearrange("p (j t) -> p j t", t=4),
+                in0=diffs[n][:].rearrange("p (j t) -> p j t", t=4),
+                in1=gain_t[:, b : b + 1, :].broadcast_to([P, UNIT, 4]),
+                op=ALU.mult,
+            )
+            hbf[n] = h
+
+        def quantize_h(n):
+            jh, u, b = units[n]
+            cols = slice(u * UNIT, (u + 1) * UNIT)
+            nc.vector.quantize_mx(out=hw[jh, b][:, cols].bitcast(FP8X4), scales=hs[jh, b][:, cols], in_=hbf[n][:])
+
+        w3q = {}
+        magnitude(0)
+        for n in range(len(units)):
+            square(n)
+            if n + 1 < len(units):
+                magnitude(n + 1)
+            nearness(n)
+            difference(n)
+            if n > 0:
+                quantize_h(n - 1)
+            apply_gain(n)
+            if n == 3:
+                w3q[0, 0] = quantize_weight(w3_raw[0][:, 0], "w3q00", nc.vector.tensor_copy, staging(ring, "grouped"))
+            if n == 4:
+                w3q[0, 1] = quantize_weight(w3_raw[0][:, 1], "w3q01", nc.vector.tensor_copy, staging(ring, "grouped"))
+        quantize_h(len(units) - 1)
+        for b in range(2):
+            w3q[1, b] = quantize_weight(w3_raw[1][:, b], "w3q1%d" % b, nc.scalar.copy, (sqs, nears)[b][1][:].bitcast(BF16))
+
+        def add_product(g, t, jh):
+            acc = psum.tile([P, BANK], F32, name="acc", bufs=2)
+            for b in range(2):
+                codes, scales = w3q[g, b]
+                nc.tensor.matmul_mx(
+                    out=acc[:],
+                    lhsT=codes[:, t * P : (t + 1) * P].bitcast(FP8X4),
+                    lhsT_scale=scales[:, t * P : (t + 1) * P],
+                    rhs=hw[jh, b][:].bitcast(FP8X4),
+                    rhs_scale=hs[jh, b][:],
+                    start=(b == 0),
+                    stop=(b == 1),
+                )
+            cols = slice(jh * BANK, (jh + 1) * BANK)
+            nc.vector.tensor_tensor(out=page[g, t][:, cols], in0=acc[:], in1=page[g, t][:, cols], op=ALU.add)
+
+        y = [keep.tile([P, 4, M], F32, name="y%d" % g) for g in range(2)]
+        y_words = [keep.tile([P, M], U32, name="y_words%d" % g, align_bytes=64) for g in range(2)]
+        y_scales = keep.tile([P, 2, M], U8, name="y_scales", align_bytes=64)
+
+        def pick(g, t, m0, m1):
+            left = ring.tile([P, m1 - m0], F32, name="left", bufs=3)
+            right = ring.tile([P, m1 - m0], F32, name="right", bufs=3)
+            nc.vector.tensor_copy(out=left[:], in_=page[g, t].indirect(pos1_t[:, m0 // 16 : m1 // 16]))
+            nc.vector.tensor_copy(out=right[:], in_=page[g, t].indirect(pos2_t[:, m0 // 16 : m1 // 16]))
+            nc.vector.tensor_tensor(out=y[g][:, t, m0:m1], in0=left[:], in1=right[:], op=ALU.max)
+            rows = out_0[g * PASS : (g + 1) * PASS, :].rearrange("(p t) m -> p t m", t=4)
+            nc.sync.dma_start(out=rows[:, t, m0:m1], in_=y[g][:, t, m0:m1])
+
+        def planes(g, m0, m1, copy):
+            y_grouped = ring.tile([P, 4 * (m1 - m0)], BF16, name="y_grouped", tag="grouped", align_bytes=64)
+            copy(
+                out=y_grouped[:].rearrange("p (c i t) -> p c t i", i=4, t=4),
+                in_=y[g][:, :, m0:m1].rearrange("p t (c i) -> p c t i", i=4),
+            )
+            nc.vector.quantize_mx(out=y_words[g][:, m0:m1].bitcast(FP8X4), scales=y_scales[:, g, m0:m1], in_=y_grouped[:])
+            words = out_1[g].rearrange("p m t -> p (m t)").bitcast(I32)
+            nc.sync.dma_start(out=words[:, m0:m1], in_=y_words[g][:, m0:m1].bitcast(I32))
+
+        for t in range(4):
+            add_product(0, t, 0)
+        for t in range(4):
+            add_product(0, t, 1)
+            pick(0, t, 0, M)
+        planes(0, 0, M, nc.scalar.copy)
+        for t in range(4):
+            add_product(1, t, 0)
+            add_product(1, t, 1)
+            if t < 3:
+                pick(1, t, 0, M)
+        pick(1, 3, 0, M // 2)
+        planes(1, 0, M // 2, nc.scalar.copy)
+        pick(1, 3, M // 2, M)
+        planes(1, M // 2, M, nc.vector.tensor_copy)
+        for q in range(4):
+            queue = nc.sync if q % 2 == 0 else nc.scalar
+            queue.dma_start(
+                out=out_2[:, 4 * q : 4 * q + 4, :].rearrange("g r m -> r g m").bitcast(I32),
+                in_=y_scales[32 * q : 32 * q + 4, :, :].bitcast(I32),
+            )

@@ -1,6 +1,7 @@
 from contextlib import ExitStack
 
 import concourse.mybir as mybir
+from concourse.masks import make_identity
 
 K, T, S, H, M, N = 512, 4096, 1024, 1024, 512, 1024
 FLOPS = 2 * (2 * K * H * S + H * N * S)
@@ -54,7 +55,12 @@ def tile_list_flank_brush_features_kernel(
         load_scale_rows(tabs, tab_scales[0], [nc.sync] * 4)
         nc.sync.dma_start(pos1_t[:], pos1)
         nc.sync.dma_start(pos2_t[:], pos2)
-        nc.gpsimd.dma_start(out=gain_t[:], in_=gain.rearrange("(b p t) -> p b t", b=2, t=4))
+        nc.scalar.dma_start(out=gain_t[:], in_=gain.rearrange("(b p t) -> p b t", b=2, t=4))
+
+        ident = keep.tile([P, P], F32, name="ident")
+        make_identity(nc, ident[:])
+        warm = keep.tile([P, 1], F32, name="warm")
+        nc.scalar.activation(out=warm[:], in_=ident[:, 0:1], func=ACT.Abs_reciprocal_sqrt, bias=1.0)
 
         def load_weight(tile, rows):
             nc.sync.dma_start(out=tile, in_=rows.rearrange("(p j) c -> p j c", j=4))
@@ -74,12 +80,12 @@ def tile_list_flank_brush_features_kernel(
         w2s = keep.tile([P, H], U8, name="w2s", align_bytes=64)
         for b in range(2):
             nc.vector.tensor_copy(
-                out=w2w[:, 2 * b * PASS : 2 * (b + 1) * PASS].rearrange("p (t m e) -> p m t e", t=4, e=2),
-                in_=w2w_raw[:, 2 * b * PASS : 2 * (b + 1) * PASS].rearrange("p (m t e) -> p m t e", t=4, e=2),
+                out=w2w[:, 2 * b * PASS : 2 * (b + 1) * PASS].rearrange("p (t m e) -> p t m e", t=4, e=2),
+                in_=w2w_raw[:, 2 * b * PASS : 2 * (b + 1) * PASS].rearrange("p (m t e) -> p t m e", t=4, e=2),
             )
         nc.vector.tensor_copy(
-            out=w2s[:].rearrange("p (b t m) -> p b m t", b=2, t=4),
-            in_=w2s_raw[:].rearrange("p (b m t) -> p b m t", b=2, t=4),
+            out=w2s[:].rearrange("p (b t m) -> p b t m", b=2, t=4),
+            in_=w2s_raw[:].rearrange("p (b m t) -> p b t m", b=2, t=4),
         )
 
         w1_raw = []
@@ -118,8 +124,9 @@ def tile_list_flank_brush_features_kernel(
         gather_table(1)
         w1q.append(quantize_weight(w1_raw[1][:], "w1q1", nc.vector.tensor_copy, staging(ring, "grouped")))
         w3_raw = [load_w3(0, "a")]
-        pages = [load_base(0, "b"), load_base(1, "c")]
-        w3_raw.append(load_w3(1, "d"))
+        pages = [load_base(0, "b")]
+        w3_raw.append(load_w3(1, "c"))
+        pages.append(load_base(1, "d"))
         page = {(g, t): pages[g][:, t * S : (t + 1) * S] for g in range(2) for t in range(4)}
 
         hw = {}
@@ -129,14 +136,24 @@ def tile_list_flank_brush_features_kernel(
                 hw[jh, b] = keep.tile([P, BANK], U32, name="hw%d%d" % (jh, b), align_bytes=64)
                 hs[jh, b] = keep.tile([P, BANK], U8, name="hs%d%d" % (jh, b), align_bytes=64)
 
-        sqs = [keep.tile([P, 4 * UNIT], F32, name="sq%d" % b, align_bytes=64) for b in range(2)]
-        nears = [keep.tile([P, 4 * UNIT], F32, name="near%d" % b, align_bytes=64) for b in range(2)]
+        lefts = [keep.tile([P, 4 * M], F32, name="left%d" % g, align_bytes=64) for g in range(2)]
+        rights = [keep.tile([P, 4 * M], F32, name="right%d" % g, align_bytes=64) for g in range(2)]
+        sqs = [rights[g][:, i * 4 * UNIT : (i + 1) * 4 * UNIT] for g in range(2) for i in range(2)]
+        nears = [lefts[g][:, i * 4 * UNIT : (i + 1) * 4 * UNIT] for g in range(2) for i in range(2)]
 
-        units = [(jh, u, b) for jh in range(2) for u in range(BANK // UNIT) for b in range(2)]
+        gain_rows = keep.tile([P, 2, 4 * UNIT], F32, name="gain_rows")
+        for b in range(2):
+            nc.scalar.copy(
+                out=gain_rows[:, b, :].rearrange("p (j t) -> p j t", t=4), in_=gain_t[:, b : b + 1, :].broadcast_to([P, UNIT, 4])
+            )
+
+        units = [(jh, j0, UNIT, b) for jh in range(2) for j0 in range(0, BANK, UNIT) for b in range(2)]
+        units[-1:] = [(1, j0, P, 1) for j0 in range(BANK - UNIT, BANK, P)]
         mags, diffs, hbf = {}, {}, {}
 
-        def blocks(u):
-            return [slice(u * UNIT + i * P, u * UNIT + (i + 1) * P) for i in range(UNIT // P)]
+        def blocks(n):
+            jh, j0, width, b = units[n]
+            return [slice(j, j + P) for j in range(j0, j0 + width, P)]
 
         def four_products(bank, words, dtype, width, scales, jh, cols):
             for t in range(4):
@@ -151,9 +168,9 @@ def tile_list_flank_brush_features_kernel(
                 )
 
         def magnitude(n):
-            jh, u, b = units[n]
-            mag = ring.tile([P, 4 * UNIT], F32, name="mag")
-            for i, cols in enumerate(blocks(u)):
+            jh, j0, width, b = units[n]
+            mag = ring.tile([P, 4 * width], F32, name="mag", bufs=3)
+            for i, cols in enumerate(blocks(n)):
                 bulge = psum.tile([P, BANK], F32, name="bulge", bufs=3)
                 four_products(bulge, w2w[:, 2 * b * PASS : 2 * (b + 1) * PASS], FP4X4, 2, w2s[:, b * PASS : (b + 1) * PASS], jh, cols)
                 nc.scalar.activation(
@@ -164,63 +181,68 @@ def tile_list_flank_brush_features_kernel(
             mags[n] = mag
 
         def square(n):
-            nc.scalar.activation(out=sqs[n % 2][:], in_=mags[n][:], func=ACT.Square, bias=1.0)
+            nc.scalar.activation(out=sqs[n % 4][:, : 4 * units[n][2]], in_=mags[n][:], func=ACT.Square, bias=1.0)
 
         def nearness(n):
-            nc.scalar.activation(out=nears[n % 2][:], in_=sqs[n % 2][:], func=ACT.Abs_reciprocal_sqrt)
+            nc.scalar.activation(out=nears[n % 4][:, : 4 * units[n][2]], in_=sqs[n % 4][:, : 4 * units[n][2]], func=ACT.Abs_reciprocal_sqrt)
 
-        def difference(n):
-            jh, u, b = units[n]
-            diff = ring.tile([P, 4 * UNIT], F32, name="diff")
+        def difference(n, i):
+            jh, j0, width, b = units[n]
+            if i == 0:
+                diffs[n] = ring.tile([P, 4 * width], F32, name="diff", bufs=3)
             codes, scales = w1q[b]
-            for i, cols in enumerate(blocks(u)):
-                reach = psum.tile([P, BANK], F32, name="reach", bufs=3)
-                four_products(reach, codes, FP8X4, 1, scales, jh, cols)
-                nc.vector.tensor_tensor(
-                    out=diff[:, i * BANK : (i + 1) * BANK].rearrange("p (j t) -> p j t", t=4),
-                    in0=reach[:].rearrange("p (t j) -> p j t", t=4),
-                    in1=nears[n % 2][:, i * BANK : (i + 1) * BANK].rearrange("p (j t) -> p j t", t=4),
-                    op=ALU.subtract,
-                )
-            diffs[n] = diff
+            reach = psum.tile([P, BANK], F32, name="reach", bufs=3)
+            four_products(reach, codes, FP8X4, 1, scales, jh, blocks(n)[i])
+            nc.vector.tensor_tensor(
+                out=diffs[n][:, i * BANK : (i + 1) * BANK].rearrange("p (j t) -> p j t", t=4),
+                in0=reach[:].rearrange("p (t j) -> p j t", t=4),
+                in1=nears[n % 4][:, i * BANK : (i + 1) * BANK].rearrange("p (j t) -> p j t", t=4),
+                op=ALU.subtract,
+            )
 
         def apply_gain(n):
-            b = units[n][2]
-            h = ring.tile([P, 4 * UNIT], BF16, name="h", align_bytes=64)
+            jh, j0, width, b = units[n]
+            h = sqs[(n + 1) % 4].bitcast(BF16)[:, : 4 * width]
             nc.vector.tensor_tensor(
-                out=h[:].rearrange("p (j t) -> p j t", t=4),
-                in0=diffs[n][:].rearrange("p (j t) -> p j t", t=4),
-                in1=gain_t[:, b : b + 1, :].broadcast_to([P, UNIT, 4]),
+                out=h,
+                in0=diffs[n][:],
+                in1=gain_rows[:, b, : 4 * width],
                 op=ALU.mult,
             )
             hbf[n] = h
 
         def quantize_h(n):
-            jh, u, b = units[n]
-            cols = slice(u * UNIT, (u + 1) * UNIT)
-            nc.vector.quantize_mx(out=hw[jh, b][:, cols].bitcast(FP8X4), scales=hs[jh, b][:, cols], in_=hbf[n][:])
+            jh, j0, width, b = units[n]
+            cols = slice(j0, j0 + width)
+            nc.vector.quantize_mx(out=hw[jh, b][:, cols].bitcast(FP8X4), scales=hs[jh, b][:, cols], in_=hbf[n])
 
         w3q = {}
+        last = len(units) - 1
         magnitude(0)
         for n in range(len(units)):
             square(n)
-            if n + 1 < len(units):
+            if n < last:
                 magnitude(n + 1)
             nearness(n)
-            difference(n)
+            difference(n, 0)
+            if n > 0:
+                apply_gain(n - 1)
+            if len(blocks(n)) > 1:
+                difference(n, 1)
+            if n == last:
+                apply_gain(n)
             if n > 0:
                 quantize_h(n - 1)
-            apply_gain(n)
             if n == 3:
-                w3q[0, 0] = quantize_weight(w3_raw[0][:, 0], "w3q00", nc.vector.tensor_copy, staging(ring, "grouped"))
+                w3q[0, 0] = quantize_weight(w3_raw[0][:, 0], "w3q00", nc.scalar.copy, staging(ring, "grouped"))
             if n == 4:
                 w3q[0, 1] = quantize_weight(w3_raw[0][:, 1], "w3q01", nc.vector.tensor_copy, staging(ring, "grouped"))
-        quantize_h(len(units) - 1)
-        for b in range(2):
-            w3q[1, b] = quantize_weight(w3_raw[1][:, b], "w3q1%d" % b, nc.scalar.copy, (sqs, nears)[b][1][:].bitcast(BF16))
+        quantize_h(last)
+        w3q[1, 1] = quantize_weight(w3_raw[1][:, 1], "w3q11", nc.scalar.copy, nears[last % 4].bitcast(BF16))
+        w3q[1, 0] = quantize_weight(w3_raw[1][:, 0], "w3q10", nc.scalar.copy, sqs[last % 4].bitcast(BF16))
 
-        def add_product(g, t, jh):
-            acc = psum.tile([P, BANK], F32, name="acc", bufs=2)
+        def product(g, t, jh, tag, bufs):
+            acc = psum.tile([P, BANK], F32, name="acc", tag=tag, bufs=bufs)
             for b in range(2):
                 codes, scales = w3q[g, b]
                 nc.tensor.matmul_mx(
@@ -232,47 +254,81 @@ def tile_list_flank_brush_features_kernel(
                     start=(b == 0),
                     stop=(b == 1),
                 )
+            return acc
+
+        def add_on_vector(g, t, jh):
             cols = slice(jh * BANK, (jh + 1) * BANK)
-            nc.vector.tensor_tensor(out=page[g, t][:, cols], in0=acc[:], in1=page[g, t][:, cols], op=ALU.add)
+            nc.vector.tensor_tensor(out=page[g, t][:, cols], in0=product(g, t, jh, *(("acc", 2), ("reach", 3))[jh])[:], in1=page[g, t][:, cols], op=ALU.add)
+
+        prods = keep.tile([P, 4 * BANK], F32, name="prods")
+        totals = keep.tile([P, 4 * BANK], F32, name="totals", align_bytes=64)
+
+        def add_on_tensor(g, t, jh):
+            half = page[g, t][:, jh * BANK : (jh + 1) * BANK]
+            slot = slice((2 * t + jh) % 4 * BANK, ((2 * t + jh) % 4 + 1) * BANK)
+            prod = prods[:, slot]
+            nc.scalar.copy(out=prod, in_=product(g, t, jh, "acc", 2)[:])
+            turned = psum.tile([P, BANK], F32, name="bulge", bufs=3)
+            for i in range(BANK // P):
+                cols = slice(i * P, (i + 1) * P)
+                nc.tensor.matmul(turned[:, cols], lhsT=half[:, cols], rhs=ident[:], start=True, stop=False, is_transpose=True)
+                nc.tensor.matmul(turned[:, cols], lhsT=prod[:, cols], rhs=ident[:], start=False, stop=True, is_transpose=True)
+            total = totals[:, slot]
+            nc.scalar.copy(out=total, in_=turned[:])
+            back = psum.tile([P, BANK], F32, name="reach", bufs=3)
+            for i in range(BANK // P):
+                cols = slice(i * P, (i + 1) * P)
+                nc.tensor.transpose(back[:, cols], total[:, cols], ident[:])
+            nc.scalar.copy(out=half, in_=back[:])
 
         y = [keep.tile([P, 4, M], F32, name="y%d" % g) for g in range(2)]
         y_words = [keep.tile([P, M], U32, name="y_words%d" % g, align_bytes=64) for g in range(2)]
         y_scales = keep.tile([P, 2, M], U8, name="y_scales", align_bytes=64)
 
-        def pick(g, t, m0, m1):
-            left = ring.tile([P, m1 - m0], F32, name="left", bufs=3)
-            right = ring.tile([P, m1 - m0], F32, name="right", bufs=3)
-            nc.vector.tensor_copy(out=left[:], in_=page[g, t].indirect(pos1_t[:, m0 // 16 : m1 // 16]))
-            nc.vector.tensor_copy(out=right[:], in_=page[g, t].indirect(pos2_t[:, m0 // 16 : m1 // 16]))
-            nc.vector.tensor_tensor(out=y[g][:, t, m0:m1], in0=left[:], in1=right[:], op=ALU.max)
-            rows = out_0[g * PASS : (g + 1) * PASS, :].rearrange("(p t) m -> p t m", t=4)
-            nc.sync.dma_start(out=rows[:, t, m0:m1], in_=y[g][:, t, m0:m1])
+        def pick(into, lst, g, t, m0, m1):
+            nc.vector.tensor_copy(out=into[g][:, t * M + m0 : t * M + m1], in_=page[g, t].indirect(lst[:, m0 // 16 : m1 // 16]))
 
-        def planes(g, m0, m1, copy):
-            y_grouped = ring.tile([P, 4 * (m1 - m0)], BF16, name="y_grouped", tag="grouped", align_bytes=64)
+        def larger(g, c0, c1):
+            flat = y[g][:].rearrange("p t m -> p (t m)")
+            nc.vector.tensor_tensor(out=flat[:, c0:c1], in0=lefts[g][:, c0:c1], in1=rights[g][:, c0:c1], op=ALU.max)
+            rows = out_0[g * PASS : (g + 1) * PASS, :].rearrange("(p t) m -> p (t m)", t=4)
+            nc.sync.dma_start(out=rows[:, c0:c1], in_=flat[:, c0:c1])
+
+        def planes(g, m0, m1, copy, stage):
+            y_grouped = stage[:, : 4 * (m1 - m0)]
             copy(
-                out=y_grouped[:].rearrange("p (c i t) -> p c t i", i=4, t=4),
+                out=y_grouped.rearrange("p (c i t) -> p c t i", i=4, t=4),
                 in_=y[g][:, :, m0:m1].rearrange("p t (c i) -> p c t i", i=4),
             )
-            nc.vector.quantize_mx(out=y_words[g][:, m0:m1].bitcast(FP8X4), scales=y_scales[:, g, m0:m1], in_=y_grouped[:])
+            nc.vector.quantize_mx(out=y_words[g][:, m0:m1].bitcast(FP8X4), scales=y_scales[:, g, m0:m1], in_=y_grouped)
             words = out_1[g].rearrange("p m t -> p (m t)").bitcast(I32)
             nc.sync.dma_start(out=words[:, m0:m1], in_=y_words[g][:, m0:m1].bitcast(I32))
 
+        for jh in range(2):
+            for t in range(4):
+                add_on_vector(0, t, jh)
         for t in range(4):
-            add_product(0, t, 0)
+            add_on_tensor(1, t, 0)
+            add_on_tensor(1, t, 1)
         for t in range(4):
-            add_product(0, t, 1)
-            pick(0, t, 0, M)
-        planes(0, 0, M, nc.scalar.copy)
-        for t in range(4):
-            add_product(1, t, 0)
-            add_product(1, t, 1)
-            if t < 3:
-                pick(1, t, 0, M)
-        pick(1, 3, 0, M // 2)
-        planes(1, 0, M // 2, nc.scalar.copy)
-        pick(1, 3, M // 2, M)
-        planes(1, M // 2, M, nc.vector.tensor_copy)
+            pick(lefts, pos1_t, 0, t, 0, M)
+            pick(rights, pos2_t, 0, t, 0, M)
+        larger(0, 0, 4 * M)
+        for t in range(3):
+            pick(lefts, pos1_t, 1, t, 0, M)
+            pick(rights, pos2_t, 1, t, 0, M)
+            if t == 1:
+                larger(1, 0, 2 * M)
+        half = M // 2
+        pick(lefts, pos1_t, 1, 3, 0, half)
+        pick(rights, pos2_t, 1, 3, 0, half)
+        pick(lefts, pos1_t, 1, 3, half, M)
+        larger(1, 2 * M, 3 * M + half)
+        pick(rights, pos2_t, 1, 3, half, M)
+        planes(0, 0, M, nc.scalar.copy, totals[:, 2 * BANK :].bitcast(BF16))
+        larger(1, 3 * M + half, 4 * M)
+        planes(1, 0, half, nc.scalar.copy, staging(ring, "grouped"))
+        planes(1, half, M, nc.vector.tensor_copy, staging(ring, "grouped"))
         for q in range(4):
             queue = nc.sync if q % 2 == 0 else nc.scalar
             queue.dma_start(

from contextlib import ExitStack

import concourse.mybir as mybir
from concourse.masks import make_identity

K, T, S, H, M, N = 512, 4096, 1024, 1024, 512, 1024
FLOPS = 2 * (2 * K * H * S + H * N * S)

F32 = mybir.dt.float32
BF16 = mybir.dt.bfloat16
I32 = mybir.dt.int32
U32 = mybir.dt.uint32
U16 = mybir.dt.uint16
U8 = mybir.dt.uint8
FP8X4 = mybir.dt.float8_e4m3fn_x4
FP4X4 = mybir.dt.float4_e2m1fn_x4
ALU = mybir.AluOpType
ACT = mybir.ActivationFunctionType

P = 128
PASS = 512
BANK = 512
UNIT = 256


def tile_list_flank_brush_features_kernel(
    tc, tab_words, tab_scales, offs, pos1, pos2, w1, w2_words, w2_scales, gain, w3, base, out_0, out_1, out_2
):
    nc = tc.nc
    with ExitStack() as ctx:
        keep = ctx.enter_context(tc.tile_pool(name="keep", bufs=1))
        big = ctx.enter_context(tc.tile_pool(name="big", bufs=1))
        ring = ctx.enter_context(tc.tile_pool(name="ring", bufs=2))
        psum = ctx.enter_context(tc.psum_pool(name="psum", bufs=1))

        def load_scale_rows(tile, rows, queues):
            for q in range(4):
                queues[q].dma_start(out=tile[32 * q : 32 * q + 4, :].bitcast(I32), in_=rows[4 * q : 4 * q + 4, :].bitcast(I32))

        offs_t = keep.tile([P, S // 16], U16, name="offs_t")
        pos1_t = keep.tile([P, M // 16], U16, name="pos1_t")
        pos2_t = keep.tile([P, M // 16], U16, name="pos2_t")
        w2s_raw = big.tile([P, H], U8, name="w2s_raw", tag="d", align_bytes=64)
        tabs = big.tile([P, T], U8, name="tabs", tag="b", align_bytes=64)
        nc.gpsimd.memset(w2s_raw[:].bitcast(I32), 0)
        nc.gpsimd.memset(tabs[:, : T // 2].bitcast(I32), 0)
        nc.vector.memset(tabs[:, T // 2 :].bitcast(I32), 0)
        w2w_raw = big.tile([P, 2 * H], U8, name="w2w_raw", tag="c", align_bytes=64)
        gain_t = keep.tile([P, 2, 4], F32, name="gain_t")
        tabw = big.tile([P, T], I32, name="tabw", tag="a", align_bytes=64)
        load_scale_rows(w2s_raw, w2_scales[0], [nc.scalar, nc.scalar, nc.scalar, nc.sync])
        nc.sync.dma_start(offs_t[:], offs)
        nc.sync.dma_start(out=w2w_raw[:].bitcast(I32), in_=w2_words[0].bitcast(I32))
        nc.sync.dma_start(out=tabw[:], in_=tab_words[0].rearrange("p n t -> p (n t)").bitcast(I32))
        load_scale_rows(tabs, tab_scales[0], [nc.sync] * 4)
        nc.sync.dma_start(pos1_t[:], pos1)
        nc.sync.dma_start(pos2_t[:], pos2)
        nc.scalar.dma_start(out=gain_t[:], in_=gain.rearrange("(b p t) -> p b t", b=2, t=4))

        ident = keep.tile([P, P], F32, name="ident")
        make_identity(nc, ident[:])
        warm = keep.tile([P, 1], F32, name="warm")
        nc.scalar.activation(out=warm[:], in_=ident[:, 0:1], func=ACT.Abs_reciprocal_sqrt, bias=1.0)

        def load_weight(tile, rows):
            nc.sync.dma_start(out=tile, in_=rows.rearrange("(p j) c -> p j c", j=4))

        def load_w3(g, tag):
            raw = big.tile([P, 2, 4, PASS], F32, name="w3_raw%d" % g, tag=tag, align_bytes=64)
            for b in range(2):
                load_weight(raw[:, b], w3[b * PASS : (b + 1) * PASS, g * PASS : (g + 1) * PASS])
            return raw

        def load_base(g, tag):
            tile = big.tile([P, 4 * S], F32, name="page%d" % g, tag=tag, align_bytes=64)
            nc.sync.dma_start(out=tile[:], in_=base[g * PASS : (g + 1) * PASS, :].rearrange("(p t) j -> p (t j)", t=4))
            return tile

        w2w = keep.tile([P, 2 * H], U8, name="w2w", align_bytes=64)
        w2s = keep.tile([P, H], U8, name="w2s", align_bytes=64)
        for b in range(2):
            nc.vector.tensor_copy(
                out=w2w[:, 2 * b * PASS : 2 * (b + 1) * PASS].rearrange("p (t m e) -> p t m e", t=4, e=2),
                in_=w2w_raw[:, 2 * b * PASS : 2 * (b + 1) * PASS].rearrange("p (m t e) -> p t m e", t=4, e=2),
            )
        nc.vector.tensor_copy(
            out=w2s[:].rearrange("p (b t m) -> p b t m", b=2, t=4),
            in_=w2s_raw[:].rearrange("p (b m t) -> p b t m", b=2, t=4),
        )

        w1_raw = []
        for b in range(2):
            raw = big.tile([P, 4, PASS], F32, name="w1_raw%d" % b, tag="cd"[b], align_bytes=64)
            load_weight(raw[:], w1[:, b * PASS : (b + 1) * PASS])
            w1_raw.append(raw)

        vw, vs = {}, {}

        def gather_table(jh):
            words = big.tile([P, BANK], U32, name="vw%d" % jh, tag="ef"[jh], align_bytes=64)
            scales = keep.tile([P, BANK], U8, name="vs%d" % jh, align_bytes=64)
            lst = offs_t[:, jh * 32 : (jh + 1) * 32]
            nc.vector.tensor_copy(out=words[:], in_=tabw[:].bitcast(U32).indirect(lst))
            nc.vector.tensor_copy(out=scales[:], in_=tabs[:].indirect(lst))
            vw[jh] = words
            vs[jh] = scales

        def staging(pool, tag):
            tile = pool.tile([P, 4 * PASS], BF16, name="grouped", tag=tag, align_bytes=64)
            return tile[:]

        def quantize_weight(raw, name, copy, grouped):
            copy(
                out=grouped.rearrange("p (t m j) -> p m j t", t=4, j=4),
                in_=raw.rearrange("p j (m t) -> p m j t", t=4),
            )
            codes = keep.tile([P, PASS], U32, name=name + "_codes", align_bytes=64)
            scales = keep.tile([P, PASS], U8, name=name + "_scales", align_bytes=64)
            nc.vector.quantize_mx(out=codes[:].bitcast(FP8X4), scales=scales[:], in_=grouped)
            return codes, scales

        gather_table(0)
        w1q = [quantize_weight(w1_raw[0][:], "w1q0", nc.vector.tensor_copy, staging(big, "f"))]
        gather_table(1)
        w1q.append(quantize_weight(w1_raw[1][:], "w1q1", nc.vector.tensor_copy, staging(ring, "grouped")))
        w3_raw = [load_w3(0, "a")]
        pages = [load_base(0, "b")]
        w3_raw.append(load_w3(1, "c"))
        pages.append(load_base(1, "d"))
        page = {(g, t): pages[g][:, t * S : (t + 1) * S] for g in range(2) for t in range(4)}

        hw = {}
        hs = {}
        for jh in range(2):
            for b in range(2):
                hw[jh, b] = keep.tile([P, BANK], U32, name="hw%d%d" % (jh, b), align_bytes=64)
                hs[jh, b] = keep.tile([P, BANK], U8, name="hs%d%d" % (jh, b), align_bytes=64)

        lefts = [keep.tile([P, 4 * M], F32, name="left%d" % g, align_bytes=64) for g in range(2)]
        rights = [keep.tile([P, 4 * M], F32, name="right%d" % g, align_bytes=64) for g in range(2)]
        sqs = [rights[g][:, i * 4 * UNIT : (i + 1) * 4 * UNIT] for g in range(2) for i in range(2)]
        nears = [lefts[g][:, i * 4 * UNIT : (i + 1) * 4 * UNIT] for g in range(2) for i in range(2)]

        gain_rows = keep.tile([P, 2, 4 * UNIT], F32, name="gain_rows")
        for b in range(2):
            nc.scalar.copy(
                out=gain_rows[:, b, :].rearrange("p (j t) -> p j t", t=4), in_=gain_t[:, b : b + 1, :].broadcast_to([P, UNIT, 4])
            )

        units = [(jh, j0, UNIT, b) for jh in range(2) for j0 in range(0, BANK, UNIT) for b in range(2)]
        units[-1:] = [(1, j0, P, 1) for j0 in range(BANK - UNIT, BANK, P)]
        mags, diffs, hbf = {}, {}, {}

        def blocks(n):
            jh, j0, width, b = units[n]
            return [slice(j, j + P) for j in range(j0, j0 + width, P)]

        def four_products(bank, words, dtype, width, scales, jh, cols):
            for t in range(4):
                nc.tensor.matmul_mx(
                    out=bank[:, t * P : (t + 1) * P],
                    lhsT=words[:, width * t * P : width * (t + 1) * P].bitcast(dtype),
                    lhsT_scale=scales[:, t * P : (t + 1) * P],
                    rhs=vw[jh][:, cols].bitcast(FP8X4),
                    rhs_scale=vs[jh][:, cols],
                    start=True,
                    stop=True,
                )

        def magnitude(n):
            jh, j0, width, b = units[n]
            mag = ring.tile([P, 4 * width], F32, name="mag", bufs=3)
            for i, cols in enumerate(blocks(n)):
                bulge = psum.tile([P, BANK], F32, name="bulge", bufs=3)
                four_products(bulge, w2w[:, 2 * b * PASS : 2 * (b + 1) * PASS], FP4X4, 2, w2s[:, b * PASS : (b + 1) * PASS], jh, cols)
                nc.scalar.activation(
                    out=mag[:, i * BANK : (i + 1) * BANK].rearrange("p (j t) -> p j t", t=4),
                    in_=bulge[:].rearrange("p (t j) -> p j t", t=4),
                    func=ACT.Abs,
                )
            mags[n] = mag

        def square(n):
            nc.scalar.activation(out=sqs[n % 4][:, : 4 * units[n][2]], in_=mags[n][:], func=ACT.Square, bias=1.0)

        def nearness(n):
            nc.scalar.activation(out=nears[n % 4][:, : 4 * units[n][2]], in_=sqs[n % 4][:, : 4 * units[n][2]], func=ACT.Abs_reciprocal_sqrt)

        def difference(n, i):
            jh, j0, width, b = units[n]
            if i == 0:
                diffs[n] = ring.tile([P, 4 * width], F32, name="diff", bufs=3)
            codes, scales = w1q[b]
            reach = psum.tile([P, BANK], F32, name="reach", bufs=3)
            four_products(reach, codes, FP8X4, 1, scales, jh, blocks(n)[i])
            nc.vector.tensor_tensor(
                out=diffs[n][:, i * BANK : (i + 1) * BANK].rearrange("p (j t) -> p j t", t=4),
                in0=reach[:].rearrange("p (t j) -> p j t", t=4),
                in1=nears[n % 4][:, i * BANK : (i + 1) * BANK].rearrange("p (j t) -> p j t", t=4),
                op=ALU.subtract,
            )

        def apply_gain(n):
            jh, j0, width, b = units[n]
            h = sqs[(n + 1) % 4].bitcast(BF16)[:, : 4 * width]
            nc.vector.tensor_tensor(
                out=h,
                in0=diffs[n][:],
                in1=gain_rows[:, b, : 4 * width],
                op=ALU.mult,
            )
            hbf[n] = h

        def quantize_h(n):
            jh, j0, width, b = units[n]
            cols = slice(j0, j0 + width)
            nc.vector.quantize_mx(out=hw[jh, b][:, cols].bitcast(FP8X4), scales=hs[jh, b][:, cols], in_=hbf[n])

        w3q = {}
        last = len(units) - 1
        magnitude(0)
        for n in range(len(units)):
            square(n)
            if n < last:
                magnitude(n + 1)
            nearness(n)
            difference(n, 0)
            if n > 0:
                apply_gain(n - 1)
            if len(blocks(n)) > 1:
                difference(n, 1)
            if n == last:
                apply_gain(n)
            if n > 0:
                quantize_h(n - 1)
            if n == 3:
                w3q[0, 0] = quantize_weight(w3_raw[0][:, 0], "w3q00", nc.scalar.copy, staging(ring, "grouped"))
            if n == 4:
                w3q[0, 1] = quantize_weight(w3_raw[0][:, 1], "w3q01", nc.vector.tensor_copy, staging(ring, "grouped"))
        quantize_h(last)
        w3q[1, 1] = quantize_weight(w3_raw[1][:, 1], "w3q11", nc.scalar.copy, nears[last % 4].bitcast(BF16))
        w3q[1, 0] = quantize_weight(w3_raw[1][:, 0], "w3q10", nc.scalar.copy, sqs[last % 4].bitcast(BF16))

        def product(g, t, jh, tag, bufs):
            acc = psum.tile([P, BANK], F32, name="acc", tag=tag, bufs=bufs)
            for b in range(2):
                codes, scales = w3q[g, b]
                nc.tensor.matmul_mx(
                    out=acc[:],
                    lhsT=codes[:, t * P : (t + 1) * P].bitcast(FP8X4),
                    lhsT_scale=scales[:, t * P : (t + 1) * P],
                    rhs=hw[jh, b][:].bitcast(FP8X4),
                    rhs_scale=hs[jh, b][:],
                    start=(b == 0),
                    stop=(b == 1),
                )
            return acc

        def add_on_vector(g, t, jh):
            cols = slice(jh * BANK, (jh + 1) * BANK)
            nc.vector.tensor_tensor(out=page[g, t][:, cols], in0=product(g, t, jh, *(("acc", 2), ("reach", 3))[jh])[:], in1=page[g, t][:, cols], op=ALU.add)

        prods = keep.tile([P, 4 * BANK], F32, name="prods")
        totals = keep.tile([P, 4 * BANK], F32, name="totals", align_bytes=64)

        def add_on_tensor(g, t, jh):
            half = page[g, t][:, jh * BANK : (jh + 1) * BANK]
            slot = slice((2 * t + jh) % 4 * BANK, ((2 * t + jh) % 4 + 1) * BANK)
            prod = prods[:, slot]
            nc.scalar.copy(out=prod, in_=product(g, t, jh, "acc", 2)[:])
            turned = psum.tile([P, BANK], F32, name="bulge", bufs=3)
            for i in range(BANK // P):
                cols = slice(i * P, (i + 1) * P)
                nc.tensor.matmul(turned[:, cols], lhsT=half[:, cols], rhs=ident[:], start=True, stop=False, is_transpose=True)
                nc.tensor.matmul(turned[:, cols], lhsT=prod[:, cols], rhs=ident[:], start=False, stop=True, is_transpose=True)
            total = totals[:, slot]
            nc.scalar.copy(out=total, in_=turned[:])
            back = psum.tile([P, BANK], F32, name="reach", bufs=3)
            for i in range(BANK // P):
                cols = slice(i * P, (i + 1) * P)
                nc.tensor.transpose(back[:, cols], total[:, cols], ident[:])
            nc.scalar.copy(out=half, in_=back[:])

        y = [keep.tile([P, 4, M], F32, name="y%d" % g) for g in range(2)]
        y_words = [keep.tile([P, M], U32, name="y_words%d" % g, align_bytes=64) for g in range(2)]
        y_scales = keep.tile([P, 2, M], U8, name="y_scales", align_bytes=64)

        def pick(into, lst, g, t, m0, m1):
            nc.vector.tensor_copy(out=into[g][:, t * M + m0 : t * M + m1], in_=page[g, t].indirect(lst[:, m0 // 16 : m1 // 16]))

        def larger(g, c0, c1):
            flat = y[g][:].rearrange("p t m -> p (t m)")
            nc.vector.tensor_tensor(out=flat[:, c0:c1], in0=lefts[g][:, c0:c1], in1=rights[g][:, c0:c1], op=ALU.max)
            rows = out_0[g * PASS : (g + 1) * PASS, :].rearrange("(p t) m -> p (t m)", t=4)
            nc.sync.dma_start(out=rows[:, c0:c1], in_=flat[:, c0:c1])

        def planes(g, m0, m1, copy, stage):
            y_grouped = stage[:, : 4 * (m1 - m0)]
            copy(
                out=y_grouped.rearrange("p (c i t) -> p c t i", i=4, t=4),
                in_=y[g][:, :, m0:m1].rearrange("p t (c i) -> p c t i", i=4),
            )
            nc.vector.quantize_mx(out=y_words[g][:, m0:m1].bitcast(FP8X4), scales=y_scales[:, g, m0:m1], in_=y_grouped)
            words = out_1[g].rearrange("p m t -> p (m t)").bitcast(I32)
            nc.sync.dma_start(out=words[:, m0:m1], in_=y_words[g][:, m0:m1].bitcast(I32))

        for jh in range(2):
            for t in range(4):
                add_on_vector(0, t, jh)
        for t in range(4):
            add_on_tensor(1, t, 0)
            add_on_tensor(1, t, 1)
        for t in range(4):
            pick(lefts, pos1_t, 0, t, 0, M)
            pick(rights, pos2_t, 0, t, 0, M)
        larger(0, 0, 4 * M)
        for t in range(3):
            pick(lefts, pos1_t, 1, t, 0, M)
            pick(rights, pos2_t, 1, t, 0, M)
            if t == 1:
                larger(1, 0, 2 * M)
        half = M // 2
        pick(lefts, pos1_t, 1, 3, 0, half)
        pick(rights, pos2_t, 1, 3, 0, half)
        pick(lefts, pos1_t, 1, 3, half, M)
        larger(1, 2 * M, 3 * M + half)
        pick(rights, pos2_t, 1, 3, half, M)
        planes(0, 0, M, nc.scalar.copy, totals[:, 2 * BANK :].bitcast(BF16))
        larger(1, 3 * M + half, 4 * M)
        planes(1, 0, half, nc.scalar.copy, staging(ring, "grouped"))
        planes(1, half, M, nc.vector.tensor_copy, staging(ring, "grouped"))
        for q in range(4):
            queue = nc.sync if q % 2 == 0 else nc.scalar
            queue.dma_start(
                out=out_2[:, 4 * q : 4 * q + 4, :].rearrange("g r m -> r g m").bitcast(I32),
                in_=y_scales[32 * q : 32 * q + 4, :, :].bitcast(I32),
            )
